import numpy as np, ml_dtypes
CORES = [1,5,17,21,33,37,49,53]
N = 8
BF = ml_dtypes.bfloat16
def gentries(a):
    return np.ascontiguousarray(a.reshape(8, 16, -1).transpose(0, 2, 1)).reshape(8, -1)
def gtable(e):
    e = np.asarray(e); return np.ascontiguousarray(e.reshape(8, -1, 16).transpose(0, 2, 1)).reshape(128, -1).astype(np.int32)
R, A, J, W, Q, SH, RO = 32, 16, 2, 4096, 45, 4, 3
def parts(rng):
    amp = rng.choice(np.array([16, 32, 64, 128]), (N, 8, 1, 1))
    p = (amp * rng.random((N, 8, 16, W))).astype(np.int64)
    s = rng.integers(0, 1009, (N, 8, 1, W)) + rng.integers(0, 16, (N, 8, 16, W))
    c = rng.integers(0, W, (N, 8, R, Q)); nbr = rng.integers(0, N * R, (N, 8, J, R)); ge = rng.integers(0, W, (N, 8, J, R))
    return p, s, c, nbr, ge
def pack(p, s, c, nbr, ge):
    return {"pe": np.ascontiguousarray(p.reshape(N, 128, W)).astype(np.float32).astype(BF), "se": np.ascontiguousarray(s.reshape(N, 128, W)).astype(np.int32),
            "cand": np.ascontiguousarray(c.reshape(N, 8, R * Q)).astype(np.int32),
            "nb": np.stack([gtable(a.reshape(8, -1)) for a in nbr]), "geo": np.stack([gtable(a.reshape(8, -1)) for a in ge])}
def setup_inputs(rng):
    return pack(*parts(rng))
def ladder():
    o = [512 + 8 * (A - 1 - a) for a in range(A)]
    w = [0] * A
    for i in range(A // 2):
        w[(A - 1 + 2 * i) % A] = 512 - 8 * i; w[2 * i] = 200 + 8 * (A // 2 - 1 - i)
    o += w[:A - 1]
    h = 512 - 8 * (A // 2 - 1); ch = [(A - 3 + 3 * i) % A for i in range(A)]; m = ch.index(A - 2)
    for i in range(A): w[ch[i]] = h - (h - 200) * i // m if i < m else 200 - 8 * (i - m)
    return np.array(o + w[:A - 3] + [w[A - 1]])
def setup_inputs_most(rng):
    p, s, c, nbr, ge = parts(rng); o = ladder(); k = W // 1024
    for q in range(N):
        for g in range(8):
            pm = rng.permutation(W); lv = np.zeros(W, np.int64); lv[pm] = np.arange(W) // k
            s[q, g] = lv[None, :]; p[q, g] = rng.integers(0, 2, (16, W))
            v = rng.integers(0, 1024, (R, Q)); v[:, :len(o)] = o[None, :] + rng.integers(-100, 301, (R, 1))
            c[q, g] = pm[v * k + rng.integers(0, k, (R, Q))]
    far = 1 + rng.permutation(N) % (N - 1)
    nbr = ((np.arange(N) + far) % N * R)[:, None, None, None] + rng.integers(0, R, (N, 8, J, R))
    return pack(p, s, c, nbr, ge)
def setup_inputs_ties(rng):
    p, s, c, nbr, ge = parts(rng)
    p[:, ::2] = rng.integers(0, 128, (N, 4, 16, 1)); p[:, 1::2] = rng.integers(0, 2, (N, 4, 16, W))
    lv = rng.integers(0, 4, (N, 8, 1, W)); lv[:, 1::2] = rng.integers(0, 12, (N, 4, 1, W))
    lone = rng.integers(0, 64, (N, 8, 1, W)) == np.arange(16)[:, None]
    s = 1 + lv + rng.integers(0, 900, (N, 8, 16, 1)) - lone
    return pack(p, s, c, nbr, ge)
def setup_inputs_ends(rng):
    p, s, c, nbr, ge = parts(rng)
    c[:, ::2] = rng.choice(np.array([0, 1, W // 2 - 1, W - 5, W - 3, W - 1]), (N, 4, R, Q)); ge[:, ::2] = rng.choice(np.array([0, 1, W - 1]), (N, 4, J, R))
    s[:, ::2, :, 0] = 0; s[:, ::2, :, W - 1] = 1023; s[:, ::2, :, W // 2 - 1] = 500
    p[:, ::4] = 127 * rng.integers(0, 2, (N, 2, 16, W))
    own = np.arange(N)[:, None, None] * R
    nbr[:, 0] = own + np.arange(R)
    nbr[:, 1] = rng.choice(np.array([0, R - 1, (N - 1) * R, N * R - 1]), (N, J, R))
    nbr[:, 3] = rng.integers(0, N * R, (N, 1, R))
    nbr[:, 5] = (own + R) % (N * R) + rng.integers(0, R, (N, J, R))
    nbr[:, 7] = own + rng.integers(0, R, (N, J, R))
    return pack(p, s, c, nbr, ge)
def setup_inputs_still(rng):
    p, s, c, nbr, ge = parts(rng); o = rng.permutation(8); b, h = o[4], o[5]
    c[:, o[4:6], ::4] = 1 << SH; nbr[:, o[4:6]] = 4 * rng.integers(0, N * R // 4, (N, 2, J, R)); ge[:, o[4:6]] = 64 * rng.integers(0, W // 64, (N, 2, J, R))
    p[:, b] = np.tile(rng.integers(0, 128, (N, 16, 64)), (1, 1, W // 64))
    s[:, b] = rng.integers(127 * J, 1016, (N, 1, W)) - J * p[:, b] + rng.integers(0, 8, (N, 16, W))
    t = np.tile(np.argsort(rng.random((N, 1, 64)), axis=-1) & 1, (1, 1, W // 64)); one = np.arange(16)[:, None] == rng.integers(0, 16, (N, 1, 1))
    p[:, h] = np.where(one, 127 * (1 - t), np.tile(rng.integers(0, 128, (N, 16, 64)), (1, 1, W // 64)))
    s[:, h] = 127 * J - J * p[:, h] + np.where(one, rng.integers(0, 101, (N, 1, 1)) + rng.integers(0, 3, (N, 1, W)), rng.integers(0, 56, (N, 1, W)) + 64 * t + rng.integers(0, 8, (N, 16, W)))
    q = int(rng.integers(0, N)); p[q] = rng.integers(0, 128, (8, 16, W)); s[q] = s[q] >> 5
    p[:, o[0]] = rng.integers(0, 128, (N, 16, 1)); s[:, o[0]] = rng.integers(0, 1024, (N, 16, 1))
    lv = rng.integers(0, 1024, (N, 1, W)); p[:, o[1]] = rng.integers(0, 2, (N, 16, W)); s[:, o[1]] = lv; s[:, o[1], int(rng.integers(0, 16))] = 1023 - lv[:, 0]
    for a in range(N):
        for g, sign in ((o[2], 1), (o[3], -1)):
            i = np.argsort(sign * s[a, g, 0][c[a, g]], axis=-1); c[a, g] = np.take_along_axis(c[a, g], i, -1)
    return pack(p, s, c, nbr, ge)
def setup_inputs_spread(rng):
    p, s, c, nbr, ge = parts(rng)
    p = np.minimum((np.exp2(7 * rng.random((N, 8, 1, W))) * rng.random((N, 8, 16, W))).astype(np.int64), 127)
    s = np.minimum((np.exp2(10 * rng.random((N, 8, 1, W))) * (0.875 + 0.125 * rng.random((N, 8, 16, W)))).astype(np.int64), 1023)
    e = rng.choice(np.array([1.0, 2.0, 4.0]), (N, 8, 1, 1))
    c = np.minimum((W * rng.random((N, 8, R, Q)) ** e).astype(np.int64), W - 1)
    nbr = np.minimum((N * R * rng.random((N, 8, J, R)) ** 2).astype(np.int64), N * R - 1)
    ge = np.minimum((W * rng.random((N, 8, J, R)) ** e).astype(np.int64), W - 1)
    return pack(p, s, c, nbr, ge)
def check_inputs(d):
    bad = []
    v = np.asarray(d["pe"]).astype(np.float32)
    if not (np.all(v >= 0) and np.all(v <= 127) and np.all(v == np.floor(v))): bad.append("range of pe")
    for k, hi in (("se", 1023), ("cand", W - 1), ("nb", N * R - 1), ("geo", W - 1)):
        if np.min(d[k]) < 0 or np.max(d[k]) > hi: bad.append("range of " + k)
    return bad
def reference(pe, se, cand, nb, geo):
    p = pe.astype(np.float32).astype(np.int32).reshape(N, 8, 16, W); s = se.astype(np.int32).reshape(N, 8, 16, W)
    qu = cand.astype(np.int64).reshape(N, 8, R, Q)
    nbl = np.stack([gentries(a) for a in nb]).astype(np.int64).reshape(N, 8, J, R); ge = np.stack([gentries(a) for a in geo]).astype(np.int64).reshape(N, 8, J, R)
    pos = np.zeros((N, 8, R, A), np.int64) + np.arange(A); head = np.full((N, 8, R, 1), A, np.int64)
    for t in range(RO):
        c = np.take_along_axis(qu, pos, 3)
        every = c.transpose(1, 0, 2, 3).reshape(8, N * R, A)
        gap = []
        for a in range(N):
            cu = every[np.arange(8)[:, None, None], nbl[a]]
            ix = (((c[a][:, None, :, :, None] * cu[:, :, :, None, :]) >> SH) + ge[a][:, :, :, None, None]) & (W - 1)
            e = np.take_along_axis(p[a], ix.reshape(8, 1, -1), 2).reshape(8, 16, J, R, A, A)
            low = np.min(e - np.roll(e, -(t + 1), axis=4), axis=5)
            own = np.take_along_axis(s[a], c[a].reshape(8, 1, -1), 2).reshape(8, 16, R, A)
            gap.append(own - np.roll(own, -(t + 1), axis=3) + np.add.reduce(low, axis=2))
        gap = np.stack(gap)
        dead = np.all(gap > 0, axis=2)
        if t < RO - 1:
            n = dead.astype(np.int64); upto = np.add.accumulate(n, axis=3)
            pos = np.where(dead, head + upto - n, pos); head = head + upto[..., -1:]
    return {"yc": np.where(dead, -1, c).reshape(N, 8, R * A).astype(np.float32), "yg": gap.reshape(N, 128, R * A).astype(np.float32)}

from concourse.bass import DstId, RemoteDMATransfer
from concourse.mybir import AluOpType, ActivationFunctionType

F32, BF, I32, U16 = "float32", "bfloat16", "int32", "uint16"
RLEN = 11 * 256
CUTS0_FIRST = (4, 10, 16)
CUTS0 = (8, 16)
CUTS1 = (4, 9, 13, 16)
INDEX_AT = 1
VSLOTS = (4, 0, 0, 0, 0, 1)

SCRATCH = {
    "nbi": ("sbuf", [128, 8], I32), "nbf": ("sbuf", [128, 8], F32), "nbs": ("sbuf", [128, 8], F32),
    "pidx": ("sbuf", [128, 4], I32), "pb": ("sbuf", [128, 8], I32), "pf": ("sbuf", [128, 8], F32), "sc": ("sbuf", [128, 8], F32),
    "ramp": ("sbuf", [128, 272], F32), "xr": ("sbuf", [128, 256], F32), "gr": ("sbuf", [128, 128], F32),
    "mask": ("sbuf", [128, 256], F32), "keep": ("sbuf", [128, 256], F32), "blk": ("sbuf", [128, 128], F32),
    "sel": ("sbuf", [128, 272], F32), "prm": ("sbuf", [128, 128], BF), "permf": ("sbuf", [128, 128], F32),
    "permn": ("sbuf", [128, 128], F32), "zz": ("sbuf", [128, 144], BF), "rr": ("sbuf", [128, RLEN], BF),
    "ones": ("sbuf", [128, 16], F32), "odup": ("sbuf", [128, 2], U16), "otr": ("sbuf", [128, 16], U16),
    "gm": ("sbuf", [128, 1024], F32), "prod": ("sbuf", [128, 512], F32), "pi": ("sbuf", [128, 512], I32),
    "posb": ("sbuf", [128, 256], BF), "dead": ("sbuf", [128, 16], F32), "tmp": ("sbuf", [128, 16], F32),
    "fs": ("sbuf", [128, 256], F32),
    "cntp": ("psum", [128, 512], F32),
}
for _s in range(2):
    for _n, _w, _d in (("pes", 4096, BF), ("ses", 4096, I32), ("ee", 8192, BF), ("dd", 8192, BF), ("mm", 8192, BF),
                       ("cw", 48, I32), ("cf", 48, F32), ("dup", 32, F32), ("offp", 16, U16), ("pp", 16, F32),
                       ("inca", 16, F32), ("incb", 16, F32), ("fm", 256, F32), ("ff", 256, F32), ("idx", 512, U16),
                       ("seo", 20, U16), ("sev", 304, F32), ("nbo", 32, U16), ("gaps", 256, F32), ("ygt", 256, F32),
                       ("yct", 16, F32), ("taba", 256, F32), ("tabb", 256, F32), ("tabc", 256, F32)):
        SCRATCH["%s%d" % (_n, _s)] = ("sbuf", [128, _w], _d)
    for _n in ("geop", "gapp", "fp"):
        SCRATCH["%s%d" % (_n, _s)] = ("psum", [128, 512], F32)

SEMAPHORES = ["cv", "cs", "cp", "cg", "sent", "lc0", "lc1", "lnb", "lpe0", "lpe1", "lse0", "lse1", "out0", "out1"] + \
             ["arr%d%d" % (s, t) for s in range(2) for t in range(3)]

A = AluOpType
COUNTER = {"v": "cv", "s": "cs", "p": "cp", "g": "cg"}


def rank_program(g, core, T, topo):
    rank = T.rank_of(core)
    if rank is None:
        return
    ops = []

    def ap(r):
        n, lo, hi = r[0], r[1], r[2]
        return T[n][:, lo:hi:r[3]] if len(r) > 3 else T[n][:, lo:hi]

    def ind(w, o):
        return ap(w).indirect(ap(o))

    def val(x):
        return ap(x) if isinstance(x, tuple) else x

    def regs(*xs):
        return [x for x in xs if isinstance(x, tuple)]

    def op(q, fn, rd, wr, acc=False, sem=None, inc=1):
        ops.append({"q": q, "fn": fn, "rd": rd, "wr": wr, "acc": acc, "sem": sem, "inc": inc})

    def copy(o, i, off=None):
        op("v", lambda: g.vector.tensor_copy(ap(o), ind(i, off) if off else ap(i)), regs(i, off), [o])

    def tt(o, a, b, f, off=None):
        op("v", lambda: g.vector.tensor_tensor(ap(o), ind(a, off) if off else ap(a), ap(b), f), regs(a, b, off), [o])

    def ts(o, a, s1, f1, s2=None, f2=None, off=None):
        def fn():
            x = ind(a, off) if off else ap(a)
            if f2 is None:
                return g.vector.tensor_scalar(ap(o), x, val(s1), None, f1)
            return g.vector.tensor_scalar(ap(o), x, val(s1), val(s2), f1, f2)
        op("v", fn, regs(a, s1, s2, off), [o])

    def scan(o, a, b, init, f0, f1):
        op("v", lambda: g.vector.tensor_tensor_scan(ap(o), ap(a), ap(b), val(init), f0, f1), regs(a, b, init), [o])

    def fill(o, c):
        op("v", lambda: g.vector.memset(ap(o), c), [], [o])

    def act(o, i, off=None, bias=None, scale=None):
        def fn():
            x = ind(i, off) if off else ap(i)
            if bias is not None:
                return g.scalar.activation(ap(o), x, ActivationFunctionType.Identity, bias=bias)
            if scale is not None:
                return g.scalar.activation(ap(o), x, ActivationFunctionType.Identity, scale=val(scale))
            return g.scalar.activation(ap(o), x, ActivationFunctionType.Identity)
        op("s", fn, regs(i, off, scale), [o])

    def mm(o, l, r, start, stop):
        op("p", lambda: g.tensor.matmul(ap(o), ap(l), ap(r), start, stop), [l, r], [o], acc=not start)

    def iota(o, pat, cm, flt):
        if flt:
            op("g", lambda: g.iota(ap(o), pat, 0, cm, allow_small_or_imprecise_dtypes=True), [], [o])
        else:
            op("g", lambda: g.iota(ap(o), pat, 0, cm), [], [o])

    def dma(q, o, i, sem, rd, wr):
        eng = g.sync if q == "y" else g.scalar
        op(q, lambda: eng.dma_start(o, i), rd, wr, sem=sem, inc=16)

    def weave(a, b):
        for i in range(max(len(a), len(b))):
            for calls in (a, b):
                if i < len(calls):
                    calls[i]()

    others = [c for c in T.cores if c != core]
    far = [c for c in others if topo.chip(c) != topo.chip(core)]
    near = [c for c in others if topo.chip(c) == topo.chip(core)]
    far_e = [e for e in topo.engines(core, far[0]) if all(e in topo.engines(core, c) for c in far)]
    near_e = [e for e in topo.engines(core, near[0]) if e not in far_e][:2]
    assert all(topo.may_write(core, c) for c in others)
    arrivals = len(far) * len(far_e) + len(near) * len(near_e)

    def tab(s, t):
        return "tab" + "abc"[t] + str(s)

    def foreign(s, t):
        return [(tab(s, t), r * 32, r * 32 + 32) for r in range(len(T.cores)) if r != rank]

    def send(s, t):
        blkr = (tab(s, t), rank * 32, rank * 32 + 32)
        sem = "arr%d%d" % (s, t)

        def fn():
            trs = []
            for dests, es in ((far, far_e), (near, near_e)):
                trs.append(RemoteDMATransfer(
                    dst_ids=[DstId(rid=topo.addr(c)[0], pnc=topo.addr(c)[1]) for c in dests],
                    dma_engine_mask=sum(1 << e for e in es), remote_sem=T.sem[sem],
                    srcs=[ap(blkr)], dsts=[ap(blkr) for c in dests]))
            g.remote_dma_fused(trs, local_sem=T.sem.sent)
            return None
        op("g", fn, [blkr], [], sem="sent", inc=len(far_e) + len(near_e))
        op("x", None, [], foreign(s, t), sem=sem, inc=arrivals)

    def n(name, s):
        return name + str(s)

    def index(s, t, j, a0=0, a1=16):
        c = (j * 256 + a0 * 16, j * 256 + a1 * 16)
        return [lambda: tt(("prod",) + c, (tab(s, t), 0, 256), (n("ff", s), a0 * 16, a1 * 16), A.mult,
                           off=(n("nbo", s), j * 16 + a0, j * 16 + a1)),
                lambda: tt(("pi",) + c, ("prod",) + c, (n("geop", s),) + c, A.add),
                lambda: ts(("pi",) + c, ("pi",) + c, 4, A.arith_shift_right, 4095, A.bitwise_and),
                lambda: copy((n("idx", s),) + c, ("pi",) + c)]

    def gather(s, j, a0, a1, q="s"):
        if a1 <= a0:
            return
        lo, hi = j * 16 + a0, j * 16 + a1
        o, w, f = (n("ee", s), lo * 256, hi * 256), (n("pes", s), 0, 4096), (n("idx", s), lo * 16, hi * 16)
        if q == "s":
            act(o, w, off=f, bias=128.0)
        else:
            ts(o, w, 128.0, A.add, off=f)

    def differ(s, j, a0, a1, d):
        for lo, hi in ((a0, min(a1, 16 - d)), (max(a0, 16 - d), a1)):
            if hi > lo:
                b = j * 16 + (lo + d) % 16
                c = ((j * 16 + lo) * 256, (j * 16 + hi) * 256)
                scan((n("dd", s),) + c, (n("ee", s),) + c, (n("ee", s), b * 256, (b + hi - lo) * 256), 0.0, A.max, A.subtract)

    def least(s, j, a0, a1):
        c = ((j * 16 + a0) * 256, (j * 16 + a1) * 256)
        scan((n("mm", s),) + c, ("rr", 0, c[1] - c[0]), (n("dd", s),) + c, 0.0, A.add, A.min)

    def self1(s):
        copy((n("seo", s), 0, 20), (n("dup", s), 0, 20))

    def self2(s, d, start):
        w = 16 + d
        copy((n("sev", s), 0, w * 16), (n("ses", s), 0, 4096), off=(n("seo", s), 0, w))
        mm((n("gapp", s), 0, 256), ("permf", 0, 128), (n("sev", s), 0, 256), start, False)
        mm((n("gapp", s), 0, 256), ("permn", 0, 128), (n("sev", s), d * 16, d * 16 + 256), False, False)

    def gap_mm(s, j, start):
        mm((n("gapp", s), 0, 256), ("prm", 0, 128), (n("mm", s), j * 4096 + 15, j * 4096 + 4096, 16), start, j == 1)

    def counts(s):
        ts(("posb", 0, 256), (n("gapp", s), 0, 256), 0.0, A.is_gt)
        for x in range(16):
            mm(("cntp", 0, 16), ("zz", 15 - x, 143 - x), ("posb", x, 256, 16), x == 0, x == 15)

    def spread(s):
        tt((n("fm", s), 0, 256), (n("cf", s), 0, 45), ("mask", 0, 256), A.mult, off=(n("offp", s), 0, 16))
        mm((n("fp", s), 0, 256), ("blk", 0, 128), (n("fm", s), 0, 256), True, True)

    def turn(s, t):
        o = (tab(s, t), rank * 32, rank * 32 + 32)
        i = (n("dup", s), 0, 32)
        op("v", lambda: g.vector.transpose(ap(o), ap(i)), [i], [o])
        send(s, t)

    def refill(s, t, between):
        inc = n("inca" if t == 0 else "incb", s)
        head = 16.0 if t == 0 else (n("inca", s), 15, 16)
        weave([lambda: ts(("dead", 0, 16), ("cntp", 0, 16), 15.5, A.is_gt),
               lambda: scan((inc, 0, 16), ("ones", 0, 16), ("dead", 0, 16), head, A.mult, A.add),
               lambda: tt(("tmp", 0, 16), ("dead", 0, 16), (inc, 0, 16), A.mult),
               lambda: tt((n("pp", s), 0, 16), (n("pp", s), 0, 16), ("tmp", 0, 16), A.max)], between)
        ts((n("offp", s), 0, 16), (n("pp", s), 0, 16), -1.0, A.add)
        spread(s)
        scan(("fs", 0, 256), ("keep", 0, 256), (n("fm", s), 0, 256), 0.0, A.mult, A.add)
        copy((n("dup", s), 0, 32), ("fs", 0, 256), off=("odup", 0, 2))
        turn(s, t + 1)

    def outputs_v(s, between):
        weave([lambda: ts(("tmp", 0, 16), ("cntp", 0, 16), -4096.0, A.mult, 65535.0, A.add),
               lambda: tt((n("yct", s), 0, 16), ("tmp", 0, 16), (n("dup", s), 0, 16), A.min)], between)
        dma("y", T.yc[4 * s:4 * s + 4, :], ap((n("yct", s), 0, 16)), n("out", s), [(n("yct", s), 0, 16)], [])

    def outputs_s(s):
        act((n("gaps", s), 0, 256), (n("gapp", s), 0, 256))
        act((n("ygt", s), 0, 256), (n("gaps", s), 0, 256), off=("otr", 0, 16))
        dma("z" if s else "y", T.yg[64 * s:64 * s + 64, :], ap((n("ygt", s), 0, 256)), n("out", s), [(n("ygt", s), 0, 256)], [])

    def load(q, src, name, s, sem, ks, after):
        for k in ks:
            for hx in range(2):
                p0, r0 = 32 * k + 16 * hx, 16 * (4 * s + k)
                dma(q, T[n(name, s)][p0:p0 + 16, :], src[r0:r0 + 16, :], sem, after, [("=" + n(name, s), 0, 4096)])

    dma("y", T.cw0[:, 0:45], T.cand[0:4, :], "lc0", [], [("cw0", 0, 45)])
    dma("z", T.cw1[:, 0:45], T.cand[4:8, :], "lc1", [], [("cw1", 0, 45)])
    dma("z", T.nbi[:, 0:4], T.nb[:, :], "lnb", [], [("nbi", 0, 4)])
    dma("z", T.nbi[:, 4:8], T.geo[:, :], "lnb", [], [("nbi", 4, 8)])
    load("y", T.pe, "pes", 0, "lpe0", (0, 1, 2), [])
    load("z", T.pe, "pes", 0, "lpe0", (3,), [])
    iota(("pidx", 0, 1), [[0, 1]], 1, False)
    iota(("ramp", 0, 272), [[1, 272]], 0, True)
    iota(("xr", 0, 256), [[0, 16], [1, 16]], 0, True)
    iota(("gr", 0, 128), [[1, 8], [0, 16]], 0, True)
    P = ("pidx", 0, 1)
    ts(("pb", 0, 1), P, 15, A.bitwise_and)
    ts(("pb", 1, 2), P, 96, A.bitwise_and)
    ts(("pb", 2, 3), P, 4, A.arith_shift_right, 1, A.bitwise_and)
    ts(("pb", 3, 4), P, 1, A.bitwise_and)
    ts(("pb", 4, 5), P, 4, A.arith_shift_right)
    fill(("rr", 0, RLEN // 2), 0.0)
    copy(("pf", 0, 5), ("pb", 0, 5))
    fill(("ones", 0, 16), 1.0)
    for s in range(2):
        copy((n("dup", s), 0, 16), (n("cw", s), 0, 16))
        copy((n("dup", s), 16, 32), (n("cw", s), 0, 16))
        turn(s, 0)
    ts(("sc", 2, 3), ("pf", 4, 5), 32.0, A.mult, ("pf", 0, 1), A.add)
    copy(("nbf", 0, 4), ("nbi", 0, 4))
    ts(("nbf", 4, 8), ("nbi", 4, 8), 16.0, A.mult, -65536.0, A.add)
    ts(("sel", 0, 272), ("ramp", 0, 272), 16.0, A.subtract, ("sc", 2, 3), A.is_equal)
    for s in range(2):
        for hx in range(2):
            c0 = 128 * s - 16 * hx + 16
            mm(("cntp", 16 + 4 * s, 20 + 4 * s), ("sel", c0, c0 + 128), ("nbf", hx, 8, 2), hx == 0, hx == 1)
    ts(("mask", 0, 256), ("xr", 0, 256), ("pf", 0, 1), A.is_equal)
    ts(("blk", 0, 128), ("gr", 0, 128), ("pf", 4, 5), A.is_equal)
    copy(("cf0", 0, 45), ("cw0", 0, 45))
    copy(("offp0", 0, 16), ("ramp", 0, 16))
    copy(("cf1", 0, 45), ("cw1", 0, 45))
    copy(("offp1", 0, 16), ("ramp", 0, 16))
    copy(("nbs", 0, 8), ("cntp", 16, 24))

    def prepare(s):
        spread(s)
        for j in range(2):
            c = (s * 512 + j * 256, s * 512 + j * 256 + 256)
            act(("gm",) + c, ("mask", 0, 256), scale=("nbs", 4 * s + 2 + j, 4 * s + 3 + j))
        mm((n("geop", s), 0, 512), ("blk", 0, 128), ("gm", s * 512, s * 512 + 512), True, True)
        act((n("ff", s), 0, 256), (n("fp", s), 0, 256))
        for j in range(2):
            ts((n("nbo", s), j * 16, j * 16 + 16), ("ones", 0, 16), ("nbs", 4 * s + j, 4 * s + j + 1), A.mult)
        ts((n("pp", s), 0, 16), ("ramp", 0, 16), 1.0, A.add)

    prepare(0)
    prepare(1)
    fill(("rr", RLEN // 2, RLEN), 0.0)
    ts(("sc", 0, 1), ("pf", 0, 1), 2.0, A.mult, ("pf", 1, 2), A.add)
    ts(("sc", 1, 2), ("pf", 3, 4), 16.0, A.mult, ("pf", 1, 2), A.add)
    ts(("sc", 3, 4), ("pf", 0, 1), 16.0, A.mult)
    fill(("rr", 0, RLEN, 16), 256.0)

    def constants():
        ts(("prm", 0, 128), ("ramp", 0, 128), ("pf", 2, 3), A.subtract, ("sc", 0, 1), A.is_equal)
        ts(("permf", 0, 128), ("ramp", 0, 128), ("pf", 2, 3), A.subtract, ("sc", 0, 1), A.is_equal)
        ts(("zz", 0, 144), ("ramp", 0, 144), 15.0, A.subtract, ("sc", 1, 2), A.is_equal)
        ts(("keep", 0, 256), ("xr", 0, 256), 0.0, A.is_gt)
        ts(("permn", 0, 128), ("permf", 0, 128), -1.0, A.mult)
        ts(("odup", 0, 2), ("ones", 0, 2), ("sc", 3, 4), A.mult, 15.0, A.add)
        ts(("otr", 0, 16), ("ramp", 0, 16), ("sc", 3, 4), A.add)

    load("y", T.pe, "pes", 1, "lpe1", range(4), foreign(0, 0)[:1])
    load("y", T.se, "ses", 0, "lse0", range(4), [])
    load("y", T.se, "ses", 1, "lse1", range(2), [])
    weave(index(0, 0, 0, 0, CUTS0_FIRST[0]), [])

    for ph in range(6):
        s, t = ph % 2, ph // 2
        o, to = 1 - s, (ph - 1) // 2
        d = t + 1
        first, last = ph == 0, ph == 5
        cuts0 = CUTS0_FIRST if first else CUTS0
        nv = VSLOTS[ph]
        gather(s, 0, 0, cuts0[0])
        ix = index(s, t, 1)
        if first:
            weave(index(0, 0, 0, cuts0[0], 16), ix)
            self1(0)
            self1(1)
            constants()
        else:
            ix[0]()
            counts(o)
            ix[1]()
            if t:
                self2(s, d, True)
            if to < 2:
                refill(o, to, ix[2:])
                self1(o)
            else:
                ix[2]()
                outputs_v(o, [ix[3]])
        if ph == 1:
            load("y", T.se, "ses", 1, "lse1", (2, 3), foreign(0, 1)[:1])
        gather(s, 1, 0, nv, "v")
        for i in range(1, len(cuts0)):
            gather(s, 0, cuts0[i - 1], cuts0[i])
        gather(s, 1, nv, CUTS1[0])
        if not first:
            if to < 2:
                act((n("ff", o), 0, 256), (n("fp", o), 0, 256))
            else:
                outputs_s(o)
        for i in range(1, len(CUTS1)):
            gather(s, 1, CUTS1[i - 1], CUTS1[i])
        parts = []
        for j, cuts in ((0, cuts0), (1, CUTS1)):
            lo = 0
            for c in cuts:
                hi = 16 if c == 16 else c - d
                parts.append((j, lo, hi))
                lo = hi
        k1 = len(cuts0)
        ki = k1 + INDEX_AT
        for i, (j, lo, hi) in enumerate(parts):
            differ(s, j, lo, hi, d)
            if 0 < i <= ki:
                least(s, *parts[i - 1])
            if i == k1:
                gap_mm(s, 0, t == 0)
            if i == ki and not last:
                ix = index(o, (ph + 1) // 2, 0)
                ix[0]()
                least(s, j, lo, hi)
                weave(ix[1:], [])
            elif i >= ki:
                least(s, j, lo, hi)
            if i == len(parts) - 2 and t == 0:
                self2(s, d, False)
        gap_mm(s, 1, False)
    counts(1)
    outputs_s(1)
    outputs_v(1, [])

    emit(g, T, ops)


def emit(g, T, ops):
    queue = {"v": g.vector, "s": g.scalar, "z": g.scalar, "p": g.tensor, "g": g, "y": g.sync}
    lane = {"v": "v", "s": "s", "z": "s", "p": "p", "g": "g", "y": "y", "x": "x"}
    total = {}
    for o in ops:
        sem = o["sem"] or COUNTER[o["q"]]
        total[sem] = total.get(sem, 0) + o["inc"]
        o["tok"] = (sem, total[sem])
    for o in ops:
        if o["sem"]:
            o["tok"] = (o["sem"], total[o["sem"]])
    known = {q: {} for q in "vspgy"}
    hist = {}

    def span(r):
        name = r[0].lstrip("=")
        if SCRATCH[name][0] == "psum":
            return name, 0, 512
        return name, r[1], r[2]

    for o in ops:
        q = lane[o["q"]]
        need = []
        mine = [(span(r), False, False) for r in o["rd"]] + [(span(r), True, r[0][0] == "=") for r in o["wr"]]
        for (name, lo, hi), w, apart in mine:
            psum = SCRATCH[name][0] == "psum"
            for p, plo, phi, pw in hist.get(name, []):
                if plo >= hi or lo >= phi or apart or q == "x":
                    continue
                same = lane[p["q"]] == q
                if not (w or pw or (psum and not same)):
                    continue
                if same and q == "p" and (o["acc"] or w):
                    continue
                need.append(p)
        for (name, lo, hi), w, apart in mine:
            hist.setdefault(name, []).append((o, lo, hi, w))
        if q == "x":
            o["clock"] = {}
            continue
        kn = known[q]
        best = {}
        for p in need:
            sem, v = p["tok"]
            if kn.get(sem, 0) < v and best.get(sem, (0, None))[0] < v:
                best[sem] = (v, p)
        for sem in list(best):
            v, p = best[sem]
            for sem2, (v2, p2) in best.items():
                if sem2 != sem and p2["clock"].get(sem, 0) >= v:
                    v = 0
            if v and kn.get(sem, 0) < v:
                queue[o["q"]].wait_ge(T.sem[sem], v)
        for sem, (v, p) in best.items():
            kn[sem] = max(kn.get(sem, 0), v)
            for k, x in p["clock"].items():
                kn[k] = max(kn.get(k, 0), x)
        o["clock"] = dict(kn)
        ins = o["fn"]()
        if ins is not None:
            ins.then_inc(T.sem[o["tok"][0]], o["inc"])
    for sem, v in total.items():
        g.sync.wait_ge(T.sem[sem], v)
